import numpy as np
import ml_dtypes


def mxq(x, axis, fmt="e4m3"):
    dtype, down = {"e4m3": (ml_dtypes.float8_e4m3fn, 7), "e5m2": (ml_dtypes.float8_e5m2, 14)}[fmt]
    v = np.moveaxis(np.asarray(x, np.float32).astype(ml_dtypes.bfloat16).astype(np.float64), axis, -1)
    blocks = v.reshape(v.shape[:-1] + (-1, 32))
    amax = np.abs(blocks).max(-1, keepdims=True)
    byte = np.maximum(np.where(amax > 0, np.frexp(amax)[1] - 1 + 127, 0) - down, 1)
    scale = np.exp2(byte - 127.0)
    codes = (blocks / scale).astype(np.float32).astype(dtype).astype(np.float64)
    return np.moveaxis((codes * scale).reshape(v.shape), -1, axis)


WIDE = False


def mx_kscale(k):
    if not WIDE:
        return np.ones(k)
    levels = np.array([10, -10, 5, -5, 0])
    if k % 512:
        return np.exp2(np.random.permutation(np.resize(levels, k // 32))).repeat(32)
    a = np.empty((k // 512, 16))
    for p in range(k // 512):
        a[p, :8] = np.random.permutation(np.resize(levels, 8))
        for g in range(8):
            far = levels[np.abs(levels - a[p, g]) >= 10]
            a[p, g + 8] = far[np.random.randint(len(far))]
    return np.exp2(a.ravel()).repeat(32)


def f64(x):
    return np.asarray(x).astype(np.float64)


def striped(idx):
    return np.tile(idx.reshape(-1, 16).T, (8, 1)).astype(np.uint16)


def unstriped(offs):
    return offs[:16].T.reshape(-1).astype(np.int64)


def striped8(idx):
    return np.concatenate([x.reshape(-1, 16).T for x in idx]).astype(np.uint16)


def runs(offs, k):
    lists = np.stack([offs[16 * r : 16 * r + 16].T.reshape(-1) for r in range(8)]).astype(np.int64)
    return lists[np.arange(k) % 512 // 64]


def pack_weight(w):
    k, n = w.shape
    w = f64(np.asarray(w, np.float32).astype(ml_dtypes.bfloat16)).reshape(k // 32, 32, n)
    amax = np.abs(w).max(1)
    byte = np.clip(np.where(amax > 0, np.frexp(amax)[1] - 1 + 127 - 7, 1), 1, 254)
    scaled = (w * np.exp2(127.0 - byte)[:, None, :]).reshape(k, n).astype(np.float32)
    words = np.ascontiguousarray(scaled.reshape(k // 512, 128, 4, n).transpose(0, 1, 3, 2)).astype(ml_dtypes.float8_e4m3fn).view(np.uint8)
    return words, np.ascontiguousarray(byte.astype(np.uint8).reshape(k // 512, 16, n))


def unpack_weight(words, scales):
    g, p, n, _ = words.shape
    vals = np.ascontiguousarray(words).view(ml_dtypes.float8_e4m3fn).astype(np.float64) * np.repeat(np.exp2(scales.astype(np.float64) - 127.0), 8, axis=1)[..., None]
    return vals.transpose(0, 1, 3, 2).reshape(g * 512, n)


K, T, S, N, H = 512, 2048, 512, 512, 512


def setup_inputs():
    n = np.random.standard_normal
    s = mx_kscale(K)[:, None]
    u = mx_kscale(H)
    packed_xT = pack_weight(n((K, T)) * s)
    return {
        "x_words": packed_xT[0],
        "x_scales": packed_xT[1],
        "w1": (n((K, H)) / np.sqrt(K) / s).astype(np.float32),
        "gn": (np.random.uniform(0.5, 1.5, (H, 1)) * u[:, None]).astype(np.float32),
        "w2": (n((H, H)) / np.sqrt(H) / u[:, None]).astype(np.float32),
        "res": n((N, S)).astype(np.float32),
        "w3": (n((H, N)) / np.sqrt(H) / u[:, None]).astype(np.float32),
        "offs": striped(np.random.permutation(T)[:S]),
        "p1": striped8(np.stack([np.random.permutation(S) for _ in range(8)])),
        "p2": striped8(np.stack([np.random.permutation(S) for _ in range(8)])),
        "p3": striped8(np.stack([np.random.permutation(S) for _ in range(8)])),
        "mv": striped8(np.stack([np.random.permutation(S) for _ in range(8)])),
    }


def reference(x_words, x_scales, w1, gn, w2, res, w3, offs, p1, p2, p3, mv):
    xq = unpack_weight(x_words, x_scales)[:, unstriped(offs)]
    y = mxq(f64(w1), 0, "e4m3").T @ xq
    x1 = y[np.arange(H)[:, None], runs(p1, H)]
    r1 = x1 / ((x1 - y) ** 2 + 1)
    x2 = y[np.arange(H)[:, None], runs(p2, H)]
    r2 = x2 / ((x2 - y) ** 2 + 1)
    x3 = y[np.arange(H)[:, None], runs(p3, H)]
    r3 = x3 / ((x3 - y) ** 2 + 1)
    z = f64(gn) * (r1 + r2 + r3)
    h = np.tanh(mxq(f64(w2), 0, "e4m3").T @ mxq(z, 0, "e4m3"))
    z2 = f64(gn) * (h[np.arange(H)[:, None], runs(mv, H)])
    return f64(res) + (mxq(f64(w3), 0, "e4m3").T @ mxq(z2, 0, "e4m3"))

@@ -1,0 +1,189 @@
+from contextlib import ExitStack
+
+import concourse.mybir as mybir
+from concourse.masks import make_identity
+
+K, T, S, N, H = 512, 2048, 512, 512, 512
+FLOPS = 3 * 2 * 512 * 512 * 512
+
+F32 = mybir.dt.float32
+BF16 = mybir.dt.bfloat16
+I32 = mybir.dt.int32
+U32 = mybir.dt.uint32
+U16 = mybir.dt.uint16
+U8 = mybir.dt.uint8
+FP8X4 = mybir.dt.float8_e4m3fn_x4
+ALU = mybir.AluOpType
+ACT = mybir.ActivationFunctionType
+
+P = 128
+PACK = 4
+CHUNKS = ((0, 256), (256, 128), (384, 128))
+TAIL = ((0, 128), (128, 128), (256, 128), (384, 128))
+
+
+def tile_picked_irls8_none_p_kernel(
+    tc, x_words, x_scales, w1, gn, w2, res, w3, offs, p1, p2, p3, mv, out
+):
+    nc = tc.nc
+    with ExitStack() as ctx:
+        keep = ctx.enter_context(tc.tile_pool(name="keep", bufs=1))
+        work = ctx.enter_context(tc.tile_pool(name="work", bufs=3))
+        psum = ctx.enter_context(tc.psum_pool(name="psum", bufs=1))
+
+        lists = [keep.tile([P, S // 16], U16, name=f"list{i}") for i in range(5)]
+        l_offs, l_p1, l_p2, l_p3, l_mv = lists
+        xw = keep.tile([P, T], U32, name="xw")
+        xs = keep.tile([P, T], U8, name="xs")
+        raw = [keep.tile([P, PACK, H], F32, name=f"raw{i}") for i in range(3)]
+        gcol = keep.tile([P, PACK], F32, name="gcol")
+        res_sb = keep.tile([P, PACK, S], F32, name="res_sb")
+        warm = keep.tile([P, 2], F32, name="warm")
+        ident = keep.tile([P, P], F32, name="ident")
+
+        nc.vector.memset(warm[:, 0:1], 1.0)
+        nc.scalar.activation(warm[:, 1:2], warm[:, 0:1], ACT.Abs_reciprocal_sqrt)
+        nc.vector.memset(xs[:].bitcast(I32), 0)
+
+        def rows4(w):
+            return w.rearrange("(p j) c -> p j c", j=PACK)
+
+        nc.sync.dma_start(raw[0][:], rows4(w1))
+        for q in range(4):
+            nc.scalar.dma_start(xs[32 * q : 32 * q + 4, :].bitcast(I32), x_scales[0, 4 * q : 4 * q + 4, :].bitcast(I32))
+        nc.sync.dma_start(xw[:].bitcast(I32), x_words[0].rearrange("p n r -> p (n r)").bitcast(I32))
+        nc.sync.dma_start(l_offs[:], offs)
+        nc.sync.dma_start(l_p1[:], p1)
+        nc.sync.dma_start(l_p2[:], p2)
+        nc.sync.dma_start(l_p3[:], p3)
+        nc.sync.dma_start(gcol[:], gn.rearrange("(p t) o -> p (t o)", t=PACK))
+        nc.sync.dma_start(raw[1][:], rows4(w2))
+        nc.sync.dma_start(l_mv[:], mv)
+        nc.sync.dma_start(raw[2][:], rows4(w3))
+        nc.sync.dma_start(res_sb[:], res.rearrange("(p t) s -> p t s", t=PACK))
+        make_identity(nc, ident[:])
+
+        wbf = [keep.tile([P, H * PACK], BF16, name=f"wbf{i}", align_bytes=64) for i in range(2)]
+        wq = [keep.tile([P, H], U32, name=f"wq{i}", align_bytes=64) for i in range(3)]
+        ws = [keep.tile([P, H], U8, name=f"ws{i}", align_bytes=64) for i in range(3)]
+
+        def dealt(i):
+            dst = wbf[i][:].rearrange("p (t m j) -> p m j t", t=PACK, j=PACK)
+            src = raw[i][:].rearrange("p j (m t) -> p m j t", t=PACK)
+            return dst, src
+
+        def quant_w(i, lo, hi):
+            nc.vector.quantize_mx(out=wq[i][:, lo:hi].bitcast(FP8X4), scales=ws[i][:, lo:hi], in_=wbf[i][:, PACK * lo : PACK * hi])
+
+        dst, src = dealt(0)
+        nc.vector.tensor_copy(dst, src)
+        xq = keep.tile([P, S], U32, name="xq", align_bytes=64)
+        xqs = keep.tile([P, S], U8, name="xqs", align_bytes=64)
+        nc.vector.tensor_copy(xqs[:], xs[:].indirect(l_offs[:]))
+        quant_w(0, 0, H)
+        nc.vector.tensor_copy(xq[:], xw[:].indirect(l_offs[:]))
+
+        def product(bank, i, t, codes, scales):
+            m = slice(P * t, P * (t + 1))
+            nc.tensor.matmul_mx(out=bank, lhsT=wq[i][:, m].bitcast(FP8X4), lhsT_scale=ws[i][:, m],
+                                rhs=codes.bitcast(FP8X4), rhs_scale=scales, start=True, stop=True)
+
+        ybank = [psum.tile([P, S], F32, name=f"row{t}") for t in range(PACK)]
+        ywin = [keep.tile([P, S], F32, name=f"ywin{t}", align_bytes=64) for t in range(PACK)]
+        for t in range(PACK):
+            product(ybank[t][:], 0, t, xq[:], xqs[:])
+            nc.scalar.copy(ywin[t][:], ybank[t][:])
+
+        gbank = psum.tile([P, PACK, P], F32, name="words")
+        for t in range(PACK):
+            nc.tensor.transpose(gbank[:, t, :], gcol[:, t : t + 1].to_broadcast([P, P]), ident[:])
+        grow = keep.tile([P, 2, P, 2], F32, name="grow")
+        nc.scalar.copy(grow[:], gbank[:].rearrange("q (u e) p -> q u p e", e=2))
+        gwide = keep.tile([P, PACK, P], F32, name="gwide")
+        nc.vector.tensor_copy(gwide[:], gcol[:].unsqueeze(2).to_broadcast([P, PACK, P]))
+
+        nc.gpsimd.tensor_copy(wbf[1][:].rearrange("p (t m j) -> p m t j", t=PACK, j=PACK),
+                              raw[1][:].rearrange("p j (m t) -> p m t j", t=PACK))
+
+        zq = keep.tile([P, S], U32, name="zq", align_bytes=64)
+        zs = keep.tile([P, S], U8, name="zs", align_bytes=64)
+        units = [(c, i) for c in range(len(CHUNKS)) for i in range(3)]
+        zbanks = {}
+        for c, i in units:
+            c0, n = CHUNKS[c]
+            last = (c, i) == units[-1]
+            x = work.tile([P, PACK, n], F32, name="x")
+            d = work.tile([P, PACK, n], F32, name="d")
+            for t in range(PACK):
+                nc.vector.tensor_copy(x[:, t, :], ywin[t][:].indirect(lists[1 + i][:, c0 // 16 : (c0 + n) // 16]))
+            for t in range(PACK):
+                nc.vector.tensor_tensor(d[:, t, :], x[:, t, :], ybank[t][:, c0 : c0 + n], ALU.subtract)
+            w = work.tile([P, PACK, n], F32, name="w")
+            r = work.tile([P, PACK, n], F32, name="r")
+            if last:
+                parts = [slice(t, t + 1) for t in range(PACK)]
+                mid = [keep.tile([P, 1, n], F32, name=f"hwin{t}")[:] for t in range(PACK)]
+            else:
+                parts = [slice(0, 2), slice(2, 4)]
+                mid = [w[:, h, :] for h in parts]
+            for h in parts:
+                nc.scalar.activation(d[:, h, :], d[:, h, :], ACT.Square)
+            for h, s in zip(parts, mid):
+                nc.scalar.activation(s, d[:, h, :], ACT.Abs_reciprocal_sqrt, bias=1.0)
+            for h, s in zip(parts, mid):
+                nc.scalar.activation(w[:, h, :], s, ACT.Square)
+            for h in parts:
+                eng = nc.vector if last else nc.gpsimd
+                eng.tensor_tensor(r[:, h, :], x[:, h, :], w[:, h, :], ALU.mult)
+            for b in range(n // P):
+                if i == 0:
+                    zbanks[c, b] = psum.tile([P, PACK, P], F32, name="zsum", bufs=3)
+                for t in range(PACK):
+                    nc.tensor.matmul(zbanks[c, b][:, t, :], r[:, t, P * b : P * (b + 1)], ident[:], is_transpose=True,
+                                     start=(i == 0 and t == 0), stop=(i == 2 and t == PACK - 1))
+            if i == 2:
+                for b in range(n // P):
+                    zt = work.tile([P, 2, P, 2], BF16, name="zt")
+                    nc.vector.tensor_tensor(zt[:], zbanks[c, b][:].rearrange("q (u e) p -> q u p e", e=2), grow[:], ALU.mult)
+                    words = zt[:].rearrange("q u p e -> q (u p e)").bitcast(F32)
+                    wb = psum.tile([P, 2, P], F32, name="words")
+                    for u in range(2):
+                        nc.tensor.transpose(wb[:, u, :], words[:, P * u : P * (u + 1)], ident[:])
+                    zg = work.tile([P, P * PACK], BF16, name="zg", align_bytes=64)
+                    nc.scalar.copy(zg[:].bitcast(F32).rearrange("p (n u) -> p n u", u=2), wb[:].rearrange("p u n -> p n u"))
+                    cols = slice(c0 + P * b, c0 + P * (b + 1))
+                    nc.vector.quantize_mx(out=zq[:, cols].bitcast(FP8X4), scales=zs[:, cols], in_=zg[:])
+            if (c, i) == (0, 2):
+                quant_w(1, 0, H)
+
+        wbf.append(keep.tile([P, H * PACK], BF16, name="ywin0", align_bytes=64))
+        dst, src = dealt(2)
+        nc.vector.tensor_copy(dst, src)
+        quant_w(2, 0, H)
+
+        abank = [psum.tile([P, S], F32, name=f"row{t}") for t in range(PACK)]
+        hwin = [keep.tile([P, S], F32, name=f"hwin{t}") for t in range(PACK)]
+        for c0, n in CHUNKS:
+            for t in range(PACK):
+                product(abank[t][:, c0 : c0 + n], 1, t, zq[:, c0 : c0 + n], zs[:, c0 : c0 + n])
+        split = CHUNKS[-1][0]
+        for lo, hi in ((0, split), (split, S)):
+            for t in range(PACK):
+                nc.scalar.activation(hwin[t][:, lo:hi], abank[t][:, lo:hi], ACT.Tanh)
+
+        out_v = out.rearrange("(p t) s -> p t s", t=PACK)
+        for c0, n in TAIL:
+            g = work.tile([P, PACK, n], F32, name="g")
+            for t in range(PACK):
+                nc.vector.tensor_tensor(g[:, t, :], hwin[t][:].indirect(l_mv[:, c0 // 16 : (c0 + n) // 16]), gwide[:, t, :], ALU.mult)
+            z2 = work.tile([P, n * PACK], BF16, name="z2", align_bytes=64)
+            nc.scalar.copy(z2[:].rearrange("p (c i t) -> p c t i", i=4, t=PACK), g[:].rearrange("p t (c i) -> p c t i", i=4))
+            q2 = work.tile([P, n], U32, name="q2", align_bytes=64)
+            s2 = work.tile([P, n], U8, name="s2", align_bytes=64)
+            nc.vector.quantize_mx(out=q2[:].bitcast(FP8X4), scales=s2[:], in_=z2[:])
+            ob = psum.tile([P, PACK, n], F32, name="zsum", bufs=3)
+            for t in range(PACK):
+                product(ob[:, t, :], 2, t, q2[:], s2[:])
+            o = work.tile([P, PACK, n], F32, name="o")
+            nc.vector.tensor_tensor(o[:], ob[:], res_sb[:, :, c0 : c0 + n], ALU.add)
+            nc.sync.dma_start(out_v[:, :, c0 : c0 + n], o[:])

@@ -18,8 +18,16 @@ ACT = mybir.ActivationFunctionType
 
 P = 128
 PACK = 4
+HALF = 256
+BLOCKS = S // P
+EARLY = S - P
+XBUFS = 4
+RING = 6
+SWITCH = 2
+WAITS = (4, 5, 4)
 CHUNKS = ((0, 256), (256, 128), (384, 128))
-TAIL = ((0, 128), (128, 128), (256, 128), (384, 128))
+TAIL = ((0, 256), (256, 128), (384, 128))
+GT = F32
 
 
 def tile_picked_irls8_none_p_kernel(
@@ -29,161 +37,243 @@ def tile_picked_irls8_none_p_kernel(
     with ExitStack() as ctx:
         keep = ctx.enter_context(tc.tile_pool(name="keep", bufs=1))
         work = ctx.enter_context(tc.tile_pool(name="work", bufs=3))
+        shared = ctx.enter_context(tc.tile_pool(name="shared", bufs=1))
         psum = ctx.enter_context(tc.psum_pool(name="psum", bufs=1))
 
         lists = [keep.tile([P, S // 16], U16, name=f"list{i}") for i in range(5)]
         l_offs, l_p1, l_p2, l_p3, l_mv = lists
         xw = keep.tile([P, T], U32, name="xw")
         xs = keep.tile([P, T], U8, name="xs")
-        raw = [keep.tile([P, PACK, H], F32, name=f"raw{i}") for i in range(3)]
+        raw1 = keep.tile([P, PACK, H], F32, name="raw1")
+        raw2 = keep.tile([P, PACK, H], F32, name="raw2")
+        raw3 = shared.tile([P, PACK, H], F32, name="raw3", offset=2048)
         gcol = keep.tile([P, PACK], F32, name="gcol")
         res_sb = keep.tile([P, PACK, S], F32, name="res_sb")
         warm = keep.tile([P, 2], F32, name="warm")
         ident = keep.tile([P, P], F32, name="ident")
 
-        nc.vector.memset(warm[:, 0:1], 1.0)
-        nc.scalar.activation(warm[:, 1:2], warm[:, 0:1], ACT.Abs_reciprocal_sqrt)
         nc.vector.memset(xs[:].bitcast(I32), 0)
+        nc.gpsimd.memset(warm[:, 0:1], 1.0)
 
         def rows4(w):
             return w.rearrange("(p j) c -> p j c", j=PACK)
 
-        nc.sync.dma_start(raw[0][:], rows4(w1))
+        nc.sync.dma_start(raw1[:], rows4(w1))
         for q in range(4):
-            nc.scalar.dma_start(xs[32 * q : 32 * q + 4, :].bitcast(I32), x_scales[0, 4 * q : 4 * q + 4, :].bitcast(I32))
-        nc.sync.dma_start(xw[:].bitcast(I32), x_words[0].rearrange("p n r -> p (n r)").bitcast(I32))
+            nc.sync.dma_start(xs[32 * q : 32 * q + 4, :].bitcast(I32), x_scales[0, 4 * q : 4 * q + 4, :].bitcast(I32))
+        nc.scalar.activation(warm[:, 1:2], warm[:, 0:1], ACT.Abs_reciprocal_sqrt)
         nc.sync.dma_start(l_offs[:], offs)
+        nc.sync.dma_start(xw[:].bitcast(I32), x_words[0].rearrange("p n r -> p (n r)").bitcast(I32))
         nc.sync.dma_start(l_p1[:], p1)
         nc.sync.dma_start(l_p2[:], p2)
         nc.sync.dma_start(l_p3[:], p3)
         nc.sync.dma_start(gcol[:], gn.rearrange("(p t) o -> p (t o)", t=PACK))
-        nc.sync.dma_start(raw[1][:], rows4(w2))
+        nc.sync.dma_start(raw2[:], rows4(w2))
+        nc.sync.dma_start(raw3[:], rows4(w3))
         nc.sync.dma_start(l_mv[:], mv)
-        nc.sync.dma_start(raw[2][:], rows4(w3))
         nc.sync.dma_start(res_sb[:], res.rearrange("(p t) s -> p t s", t=PACK))
         make_identity(nc, ident[:])
 
         wbf = [keep.tile([P, H * PACK], BF16, name=f"wbf{i}", align_bytes=64) for i in range(2)]
-        wq = [keep.tile([P, H], U32, name=f"wq{i}", align_bytes=64) for i in range(3)]
+        wq = [keep.tile([P, H], U32, name="wq0", align_bytes=64)]
         ws = [keep.tile([P, H], U8, name=f"ws{i}", align_bytes=64) for i in range(3)]
 
-        def dealt(i):
-            dst = wbf[i][:].rearrange("p (t m j) -> p m j t", t=PACK, j=PACK)
-            src = raw[i][:].rearrange("p j (m t) -> p m j t", t=PACK)
-            return dst, src
+        def dealt(dst, src, first, lo, hi):
+            return (dst[:].rearrange("p (t m j) -> p m t j", t=PACK, j=PACK)[:, first + lo : first + hi],
+                    src[:].rearrange("p j (m t) -> p m t j", t=PACK)[:, lo:hi])
 
-        def quant_w(i, lo, hi):
-            nc.vector.quantize_mx(out=wq[i][:, lo:hi].bitcast(FP8X4), scales=ws[i][:, lo:hi], in_=wbf[i][:, PACK * lo : PACK * hi])
+        def quant_w(i):
+            nc.vector.quantize_mx(out=wq[i][:].bitcast(FP8X4), scales=ws[i][:], in_=wbf[i][:])
 
-        dst, src = dealt(0)
-        nc.vector.tensor_copy(dst, src)
-        xq = keep.tile([P, S], U32, name="xq", align_bytes=64)
-        xqs = keep.tile([P, S], U8, name="xqs", align_bytes=64)
-        nc.vector.tensor_copy(xqs[:], xs[:].indirect(l_offs[:]))
-        quant_w(0, 0, H)
-        nc.vector.tensor_copy(xq[:], xw[:].indirect(l_offs[:]))
+        def bank(tag, shape):
+            return psum.tile(shape, F32, name=tag)
 
-        def product(bank, i, t, codes, scales):
+        def turn(dst, src, start, stop):
+            nc.tensor.matmul(dst, src, ident[:], is_transpose=True, start=start, stop=stop)
+
+        def product(dst, i, t, codes, scales):
             m = slice(P * t, P * (t + 1))
-            nc.tensor.matmul_mx(out=bank, lhsT=wq[i][:, m].bitcast(FP8X4), lhsT_scale=ws[i][:, m],
+            nc.tensor.matmul_mx(out=dst, lhsT=wq[i][:, m].bitcast(FP8X4), lhsT_scale=ws[i][:, m],
                                 rhs=codes.bitcast(FP8X4), rhs_scale=scales, start=True, stop=True)
 
-        ybank = [psum.tile([P, S], F32, name=f"row{t}") for t in range(PACK)]
+        xq = keep.tile([P, S], U32, name="xq", align_bytes=64)
+        xqs = keep.tile([P, S], U8, name="xqs", align_bytes=64)
+        nc.vector.tensor_copy(*dealt(wbf[0], raw1, 0, 0, 80))
+        nc.scalar.copy(*dealt(wbf[0], raw1, 0, 80, P))
+        nc.vector.tensor_copy(xqs[:], xs[:].indirect(l_offs[:]))
+        quant_w(0)
+        for lo in (0, HALF):
+            nc.vector.tensor_copy(xq[:, lo : lo + HALF], xw[:].indirect(l_offs[:, lo // 16 : (lo + HALF) // 16]))
+
         ywin = [keep.tile([P, S], F32, name=f"ywin{t}", align_bytes=64) for t in range(PACK)]
+        ybank = {(u, v): bank(f"y{2 * u + v}", [P, 2, HALF]) for v in range(2) for u in range(2)}
+        for v in range(2):
+            for u in range(2):
+                cols = slice(HALF * u, HALF * (u + 1))
+                for e in range(2):
+                    product(ybank[u, v][:, e, :], 0, 2 * v + e, xq[:, cols], xqs[:, cols])
         for t in range(PACK):
-            product(ybank[t][:], 0, t, xq[:], xqs[:])
-            nc.scalar.copy(ywin[t][:], ybank[t][:])
+            for u in range(2):
+                copy = nc.vector.tensor_copy if (t, u) == (1, 0) else nc.scalar.copy
+                copy(ywin[t][:, HALF * u : HALF * (u + 1)], ybank[u, t // 2][:, t % 2, :])
 
-        gbank = psum.tile([P, PACK, P], F32, name="words")
+        gbank = bank("s2", [P, PACK, P])
         for t in range(PACK):
-            nc.tensor.transpose(gbank[:, t, :], gcol[:, t : t + 1].to_broadcast([P, P]), ident[:])
+            turn(gbank[:, t, :], gcol[:, t : t + 1].to_broadcast([P, P]), True, True)
         grow = keep.tile([P, 2, P, 2], F32, name="grow")
-        nc.scalar.copy(grow[:], gbank[:].rearrange("q (u e) p -> q u p e", e=2))
-        gwide = keep.tile([P, PACK, P], F32, name="gwide")
-        nc.vector.tensor_copy(gwide[:], gcol[:].unsqueeze(2).to_broadcast([P, PACK, P]))
-
-        nc.gpsimd.tensor_copy(wbf[1][:].rearrange("p (t m j) -> p m t j", t=PACK, j=PACK),
-                              raw[1][:].rearrange("p j (m t) -> p m t j", t=PACK))
+        wbf.append(keep.tile([P, H * PACK], BF16, name="wbf2", align_bytes=64))
+        for i, raw in ((1, raw2), (2, raw3)):
+            for lo in (0, 64):
+                nc.gpsimd.tensor_copy(*dealt(wbf[i], raw, 0, lo, lo + 64))
 
         zq = keep.tile([P, S], U32, name="zq", align_bytes=64)
         zs = keep.tile([P, S], U8, name="zs", align_bytes=64)
-        units = [(c, i) for c in range(len(CHUNKS)) for i in range(3)]
-        zbanks = {}
-        for c, i in units:
-            c0, n = CHUNKS[c]
-            last = (c, i) == units[-1]
-            x = work.tile([P, PACK, n], F32, name="x")
-            d = work.tile([P, PACK, n], F32, name="d")
-            for t in range(PACK):
-                nc.vector.tensor_copy(x[:, t, :], ywin[t][:].indirect(lists[1 + i][:, c0 // 16 : (c0 + n) // 16]))
-            for t in range(PACK):
-                nc.vector.tensor_tensor(d[:, t, :], x[:, t, :], ybank[t][:, c0 : c0 + n], ALU.subtract)
-            w = work.tile([P, PACK, n], F32, name="w")
-            r = work.tile([P, PACK, n], F32, name="r")
+        units = [(c0, n, t, (0, 1, 2)) for c0, n in CHUNKS for t in range(PACK)]
+        units[-1:] = [(EARLY, P, PACK - 1, (i,)) for i in range(3)]
+        sums = ["s0", "s1", "y0"]
+        backs = ["s2", "s3", "y1"]
+        zbank = {}
+        zlast = keep.tile([P, PACK, P], BF16, name="zplanes")
+
+        def quant_z(b, zg):
+            cols = slice(P * b, P * (b + 1))
+            nc.vector.quantize_mx(out=zq[:, cols].bitcast(FP8X4), scales=zs[:, cols], in_=zg[:])
+
+        def finish(b):
+            zt = work.tile([P, 2, P, 2], BF16, name="zt")
+            nc.vector.tensor_tensor(zt[:], zbank[b][:].rearrange("q (u e) p -> q u p e", e=2), grow[:], ALU.mult)
+            words = zt[:].rearrange("q u p e -> q (u p e)").bitcast(F32)
+            back = bank(backs[b], [P, 2, P])
+            for u in range(2):
+                turn(back[:, u, :], words[:, P * u : P * (u + 1)], True, True)
+            return back
+
+        def pack(b, back, tag):
+            zg = keep.tile([P, P * PACK], BF16, name=tag, align_bytes=64)
+            nc.scalar.copy(zg[:].bitcast(F32).rearrange("p (n u) -> p n u", u=2), back[:].rearrange("p u n -> p n u"))
+            quant_z(b, zg)
+
+        def gate(k):
+            if k == 0:
+                return "first"
+            if k <= SWITCH:
+                return f"ring{(k - 1) % RING}"
+            if k == SWITCH + 1:
+                return f"tie{SWITCH - 1}"
+            return f"ring{(k - 2) % RING}"
+
+        later = {}
+        small = []
+        for k, (c0, n, t, near) in enumerate(units):
+            m = len(near)
+            last = k == len(units) - 1
+            direct = c0 == EARLY
+            x = keep.tile([P, m, n], F32, name=gate(k), align_bytes=64)
+            w = work.tile([P, m, n], F32, name="w", bufs=XBUFS)
+            groups = [(0, 1), (2,)] if m > 1 and n == P else [(j,) for j in range(m)]
+            tags = [f"ring{k % RING}", f"mid{k % 2}", f"tie{k}"] if len(groups) == 3 else [f"ring{k % RING}", f"tie{k}"][: len(groups)]
+            d = [keep.tile([P, len(g), n], F32, name=tag, align_bytes=64) for g, tag in zip(groups, tags)]
+            own = ybank[c0 // HALF, t // 2][:, t % 2, c0 % HALF : c0 % HALF + n]
+            for g, dg in zip(groups, d):
+                for e, j in enumerate(g):
+                    nc.vector.tensor_copy(x[:, j, :], ywin[t][:].indirect(lists[1 + near[j]][:, c0 // 16 : (c0 + n) // 16]))
+                    nc.vector.tensor_tensor(dg[:, e, :], x[:, j, :], own, ALU.subtract)
+            for b, back, tag in later.get(k, []):
+                pack(b, back, tag)
+            parts = [slice(g[0], g[-1] + 1) for g in groups]
+            for part, dg in zip(parts, d):
+                nc.scalar.activation(w[:, part, :], dg[:], ACT.Square)
             if last:
-                parts = [slice(t, t + 1) for t in range(PACK)]
-                mid = [keep.tile([P, 1, n], F32, name=f"hwin{t}")[:] for t in range(PACK)]
+                root = [keep.tile([P, P // PACK], F32, name=f"hwin{q}") for q in range(PACK)]
+                for q in range(PACK):
+                    nc.scalar.activation(root[q][:], w[:, 0, 32 * q : 32 * (q + 1)], ACT.Abs_reciprocal_sqrt, bias=1.0)
+                for q in range(PACK):
+                    nc.scalar.activation(w[:, 0, 32 * q : 32 * (q + 1)], root[q][:], ACT.Square)
             else:
-                parts = [slice(0, 2), slice(2, 4)]
-                mid = [w[:, h, :] for h in parts]
-            for h in parts:
-                nc.scalar.activation(d[:, h, :], d[:, h, :], ACT.Square)
-            for h, s in zip(parts, mid):
-                nc.scalar.activation(s, d[:, h, :], ACT.Abs_reciprocal_sqrt, bias=1.0)
-            for h, s in zip(parts, mid):
-                nc.scalar.activation(w[:, h, :], s, ACT.Square)
-            for h in parts:
-                eng = nc.vector if last else nc.gpsimd
-                eng.tensor_tensor(r[:, h, :], x[:, h, :], w[:, h, :], ALU.mult)
-            for b in range(n // P):
-                if i == 0:
-                    zbanks[c, b] = psum.tile([P, PACK, P], F32, name="zsum", bufs=3)
-                for t in range(PACK):
-                    nc.tensor.matmul(zbanks[c, b][:, t, :], r[:, t, P * b : P * (b + 1)], ident[:], is_transpose=True,
-                                     start=(i == 0 and t == 0), stop=(i == 2 and t == PACK - 1))
-            if i == 2:
-                for b in range(n // P):
-                    zt = work.tile([P, 2, P, 2], BF16, name="zt")
-                    nc.vector.tensor_tensor(zt[:], zbanks[c, b][:].rearrange("q (u e) p -> q u p e", e=2), grow[:], ALU.mult)
-                    words = zt[:].rearrange("q u p e -> q (u p e)").bitcast(F32)
-                    wb = psum.tile([P, 2, P], F32, name="words")
-                    for u in range(2):
-                        nc.tensor.transpose(wb[:, u, :], words[:, P * u : P * (u + 1)], ident[:])
-                    zg = work.tile([P, P * PACK], BF16, name="zg", align_bytes=64)
-                    nc.scalar.copy(zg[:].bitcast(F32).rearrange("p (n u) -> p n u", u=2), wb[:].rearrange("p u n -> p n u"))
-                    cols = slice(c0 + P * b, c0 + P * (b + 1))
-                    nc.vector.quantize_mx(out=zq[:, cols].bitcast(FP8X4), scales=zs[:, cols], in_=zg[:])
-            if (c, i) == (0, 2):
-                quant_w(1, 0, H)
+                for part in parts:
+                    nc.scalar.activation(w[:, part, :], w[:, part, :], ACT.Abs_reciprocal_sqrt, bias=1.0)
+                for part in parts:
+                    nc.scalar.activation(w[:, part, :], w[:, part, :], ACT.Square)
+            r = shared.tile([P, m, n], F32, name=f"r{k}", offset=3072 * k) if k < PACK else work.tile([P, m, n], F32, name="r", bufs=XBUFS)
+            gain = gcol[:, t : t + 1]
+            if not direct:
+                for part in parts if n > P else [slice(0, m)]:
+                    nc.gpsimd.tensor_tensor(r[:, part, :], x[:, part, :], w[:, part, :], ALU.mult)
+                for b in range(c0 // P, (c0 + n) // P):
+                    if t == 0:
+                        zbank[b] = bank(sums[b], [P, PACK, P])
+                    for i in near:
+                        turn(zbank[b][:, t, :], r[:, i, P * b - c0 : P * (b + 1) - c0], i == 0, i == 2)
+                    if t == PACK - 1:
+                        wait = WAITS[b]
+                        later.setdefault(k + wait + 1, []).append((b, finish(b), f"tie{k + wait}"))
+            elif m > 1:
+                two = work.tile([P, n], F32, name="two")
+                pair = keep.tile([P, 2, n], F32, name=f"pair{t}", align_bytes=64)
+                nc.gpsimd.tensor_tensor(pair[:], x[:, 0:2, :], w[:, 0:2, :], ALU.mult)
+                nc.gpsimd.tensor_tensor(two[:], pair[:, 0, :], pair[:, 1, :], ALU.add)
+                nc.vector.scalar_tensor_tensor(r[:, 2, :], x[:, 2, :], gain, w[:, 2, :], ALU.mult, ALU.mult)
+                nc.vector.scalar_tensor_tensor(zlast[:, t, :], two[:], gain, r[:, 2, :], ALU.mult, ALU.add)
+            else:
+                nc.vector.scalar_tensor_tensor(r[:, 0, :], x[:, 0, :], gain, w[:, 0, :], ALU.mult, ALU.mult)
+                small.append(r)
+                if near[0] == 1:
+                    two = work.tile([P, n], F32, name="two")
+                    nc.vector.tensor_tensor(two[:], small[0][:, 0, :], small[1][:, 0, :], ALU.add)
+                if last:
+                    nc.vector.tensor_tensor(zlast[:, t, :], two[:], r[:, 0, :], ALU.add)
+            if k == 1:
+                nc.scalar.copy(grow[:], gbank[:].rearrange("q (u e) p -> q u p e", e=2))
 
-        wbf.append(keep.tile([P, H * PACK], BF16, name="ywin0", align_bytes=64))
-        dst, src = dealt(2)
-        nc.vector.tensor_copy(dst, src)
-        quant_w(2, 0, H)
+        wq.append(keep.tile([P, H], U32, name="ywin3", align_bytes=64))
+        quant_w(1)
+        zg = keep.tile([P, P * PACK], BF16, name="zlast", align_bytes=64)
+        nc.vector.tensor_copy(zg[:].rearrange("p (c i t) -> p c t i", i=4, t=PACK), zlast[:].rearrange("p t (c i) -> p c t i", i=4))
+        quant_z(BLOCKS - 1, zg)
+        wq.append(keep.tile([P, H], U32, name="zlast", align_bytes=64))
 
-        abank = [psum.tile([P, S], F32, name=f"row{t}") for t in range(PACK)]
+        abank = [bank(f"s{t}", [P, EARLY]) for t in range(PACK)]
         hwin = [keep.tile([P, S], F32, name=f"hwin{t}") for t in range(PACK)]
-        for c0, n in CHUNKS:
-            for t in range(PACK):
-                product(abank[t][:, c0 : c0 + n], 1, t, zq[:, c0 : c0 + n], zs[:, c0 : c0 + n])
-        split = CHUNKS[-1][0]
-        for lo, hi in ((0, split), (split, S)):
-            for t in range(PACK):
-                nc.scalar.activation(hwin[t][:, lo:hi], abank[t][:, lo:hi], ACT.Tanh)
+        for t in range(PACK):
+            for lo, hi in ((0, HALF), (HALF, EARLY)):
+                product(abank[t][:, lo:hi], 1, t, zq[:, lo:hi], zs[:, lo:hi])
+        late = bank("y0", [P, PACK, P])
+        hlate = keep.tile([P, PACK, P], F32, name="g1")
+        for t in range(PACK):
+            product(late[:, t, :], 1, t, zq[:, EARLY:S], zs[:, EARLY:S])
+        for t in range(PACK):
+            nc.scalar.activation(hwin[t][:, 0:EARLY], abank[t][:], ACT.Tanh)
+        for t in range(PACK):
+            nc.scalar.activation(hlate[:, t, :], late[:, t, :], ACT.Tanh)
+        for t in range(PACK):
+            nc.vector.tensor_scalar(hwin[t][:, 0:EARLY], hwin[t][:, 0:EARLY], gcol[:, t : t + 1], None, ALU.mult)
+        quant_w(2)
+        for t in range(PACK):
+            nc.vector.tensor_scalar(hwin[t][:, EARLY:S], hlate[:, t, :], gcol[:, t : t + 1], None, ALU.mult)
 
         out_v = out.rearrange("(p t) s -> p t s", t=PACK)
-        for c0, n in TAIL:
-            g = work.tile([P, PACK, n], F32, name="g")
+        obank = []
+        tags = ["y1", "y2", "y3", "s0", "s1", "s2"]
+        for c, (c0, n) in enumerate(TAIL):
+            g = keep.tile([P, PACK, n], GT, name=f"g{c % 2}")
             for t in range(PACK):
-                nc.vector.tensor_tensor(g[:, t, :], hwin[t][:].indirect(l_mv[:, c0 // 16 : (c0 + n) // 16]), gwide[:, t, :], ALU.mult)
-            z2 = work.tile([P, n * PACK], BF16, name="z2", align_bytes=64)
-            nc.scalar.copy(z2[:].rearrange("p (c i t) -> p c t i", i=4, t=PACK), g[:].rearrange("p t (c i) -> p c t i", i=4))
-            q2 = work.tile([P, n], U32, name="q2", align_bytes=64)
-            s2 = work.tile([P, n], U8, name="s2", align_bytes=64)
-            nc.vector.quantize_mx(out=q2[:].bitcast(FP8X4), scales=s2[:], in_=z2[:])
-            ob = psum.tile([P, PACK, n], F32, name="zsum", bufs=3)
-            for t in range(PACK):
-                product(ob[:, t, :], 2, t, q2[:], s2[:])
-            o = work.tile([P, PACK, n], F32, name="o")
-            nc.vector.tensor_tensor(o[:], ob[:], res_sb[:, :, c0 : c0 + n], ALU.add)
-            nc.sync.dma_start(out_v[:, :, c0 : c0 + n], o[:])
+                nc.vector.tensor_copy(g[:, t, :], hwin[t][:].indirect(l_mv[:, c0 // 16 : (c0 + n) // 16]))
+            for b in range(c0 // P, (c0 + n) // P):
+                final = b == BLOCKS - 1
+                z2 = work.tile([P, P * PACK], BF16, name="z2", align_bytes=64)
+                weave = nc.vector.tensor_copy if final else nc.scalar.copy
+                weave(z2[:].rearrange("p (c i t) -> p c t i", i=4, t=PACK),
+                      g[:, :, P * b - c0 : P * (b + 1) - c0].rearrange("p t (c i) -> p c t i", i=4))
+                q2 = work.tile([P, P], U32, name="q2", align_bytes=64)
+                s2 = work.tile([P, P], U8, name="s2", align_bytes=64)
+                nc.vector.quantize_mx(out=q2[:].bitcast(FP8X4), scales=s2[:], in_=z2[:])
+                rows = 2 if final else PACK
+                for t0 in range(0, PACK, rows):
+                    ob = bank(tags[len(obank)], [P, rows, P])
+                    obank.append((ob, slice(t0, t0 + rows), slice(P * b, P * (b + 1))))
+                    for t in range(rows):
+                        product(ob[:, t, :], 2, t0 + t, q2[:], s2[:])
+        for ob, planes, cols in obank:
+            o = work.tile([P, planes.stop - planes.start, cols.stop - cols.start], F32, name="o", bufs=6)
+            nc.vector.tensor_tensor(o[:], ob[:], res_sb[:, planes, cols], ALU.add)
+            nc.sync.dma_start(out_v[:, planes, cols], o[:])

from contextlib import ExitStack

import concourse.mybir as mybir
from concourse.masks import make_identity

K, T, S, N, H = 512, 2048, 512, 512, 512
FLOPS = 3 * 2 * 512 * 512 * 512

F32 = mybir.dt.float32
BF16 = mybir.dt.bfloat16
I32 = mybir.dt.int32
U32 = mybir.dt.uint32
U16 = mybir.dt.uint16
U8 = mybir.dt.uint8
FP8X4 = mybir.dt.float8_e4m3fn_x4
ALU = mybir.AluOpType
ACT = mybir.ActivationFunctionType

P = 128
PACK = 4
HALF = 256
BLOCKS = S // P
EARLY = S - P
XBUFS = 4
RING = 6
SWITCH = 2
WAITS = (4, 5, 4)
CHUNKS = ((0, 256), (256, 128), (384, 128))
TAIL = ((0, 256), (256, 128), (384, 128))
GT = F32


def tile_picked_irls8_none_p_kernel(
    tc, x_words, x_scales, w1, gn, w2, res, w3, offs, p1, p2, p3, mv, out
):
    nc = tc.nc
    with ExitStack() as ctx:
        keep = ctx.enter_context(tc.tile_pool(name="keep", bufs=1))
        work = ctx.enter_context(tc.tile_pool(name="work", bufs=3))
        shared = ctx.enter_context(tc.tile_pool(name="shared", bufs=1))
        psum = ctx.enter_context(tc.psum_pool(name="psum", bufs=1))

        lists = [keep.tile([P, S // 16], U16, name=f"list{i}") for i in range(5)]
        l_offs, l_p1, l_p2, l_p3, l_mv = lists
        xw = keep.tile([P, T], U32, name="xw")
        xs = keep.tile([P, T], U8, name="xs")
        raw1 = keep.tile([P, PACK, H], F32, name="raw1")
        raw2 = keep.tile([P, PACK, H], F32, name="raw2")
        raw3 = shared.tile([P, PACK, H], F32, name="raw3", offset=2048)
        gcol = keep.tile([P, PACK], F32, name="gcol")
        res_sb = keep.tile([P, PACK, S], F32, name="res_sb")
        warm = keep.tile([P, 2], F32, name="warm")
        ident = keep.tile([P, P], F32, name="ident")

        nc.vector.memset(xs[:].bitcast(I32), 0)
        nc.gpsimd.memset(warm[:, 0:1], 1.0)

        def rows4(w):
            return w.rearrange("(p j) c -> p j c", j=PACK)

        nc.sync.dma_start(raw1[:], rows4(w1))
        for q in range(4):
            nc.sync.dma_start(xs[32 * q : 32 * q + 4, :].bitcast(I32), x_scales[0, 4 * q : 4 * q + 4, :].bitcast(I32))
        nc.scalar.activation(warm[:, 1:2], warm[:, 0:1], ACT.Abs_reciprocal_sqrt)
        nc.sync.dma_start(l_offs[:], offs)
        nc.sync.dma_start(xw[:].bitcast(I32), x_words[0].rearrange("p n r -> p (n r)").bitcast(I32))
        nc.sync.dma_start(l_p1[:], p1)
        nc.sync.dma_start(l_p2[:], p2)
        nc.sync.dma_start(l_p3[:], p3)
        nc.sync.dma_start(gcol[:], gn.rearrange("(p t) o -> p (t o)", t=PACK))
        nc.sync.dma_start(raw2[:], rows4(w2))
        nc.sync.dma_start(raw3[:], rows4(w3))
        nc.sync.dma_start(l_mv[:], mv)
        nc.sync.dma_start(res_sb[:], res.rearrange("(p t) s -> p t s", t=PACK))
        make_identity(nc, ident[:])

        wbf = [keep.tile([P, H * PACK], BF16, name=f"wbf{i}", align_bytes=64) for i in range(2)]
        wq = [keep.tile([P, H], U32, name="wq0", align_bytes=64)]
        ws = [keep.tile([P, H], U8, name=f"ws{i}", align_bytes=64) for i in range(3)]

        def dealt(dst, src, first, lo, hi):
            return (dst[:].rearrange("p (t m j) -> p m t j", t=PACK, j=PACK)[:, first + lo : first + hi],
                    src[:].rearrange("p j (m t) -> p m t j", t=PACK)[:, lo:hi])

        def quant_w(i):
            nc.vector.quantize_mx(out=wq[i][:].bitcast(FP8X4), scales=ws[i][:], in_=wbf[i][:])

        def bank(tag, shape):
            return psum.tile(shape, F32, name=tag)

        def turn(dst, src, start, stop):
            nc.tensor.matmul(dst, src, ident[:], is_transpose=True, start=start, stop=stop)

        def product(dst, i, t, codes, scales):
            m = slice(P * t, P * (t + 1))
            nc.tensor.matmul_mx(out=dst, lhsT=wq[i][:, m].bitcast(FP8X4), lhsT_scale=ws[i][:, m],
                                rhs=codes.bitcast(FP8X4), rhs_scale=scales, start=True, stop=True)

        xq = keep.tile([P, S], U32, name="xq", align_bytes=64)
        xqs = keep.tile([P, S], U8, name="xqs", align_bytes=64)
        nc.vector.tensor_copy(*dealt(wbf[0], raw1, 0, 0, 80))
        nc.scalar.copy(*dealt(wbf[0], raw1, 0, 80, P))
        nc.vector.tensor_copy(xqs[:], xs[:].indirect(l_offs[:]))
        quant_w(0)
        for lo in (0, HALF):
            nc.vector.tensor_copy(xq[:, lo : lo + HALF], xw[:].indirect(l_offs[:, lo // 16 : (lo + HALF) // 16]))

        ywin = [keep.tile([P, S], F32, name=f"ywin{t}", align_bytes=64) for t in range(PACK)]
        ybank = {(u, v): bank(f"y{2 * u + v}", [P, 2, HALF]) for v in range(2) for u in range(2)}
        for v in range(2):
            for u in range(2):
                cols = slice(HALF * u, HALF * (u + 1))
                for e in range(2):
                    product(ybank[u, v][:, e, :], 0, 2 * v + e, xq[:, cols], xqs[:, cols])
        for t in range(PACK):
            for u in range(2):
                copy = nc.vector.tensor_copy if (t, u) == (1, 0) else nc.scalar.copy
                copy(ywin[t][:, HALF * u : HALF * (u + 1)], ybank[u, t // 2][:, t % 2, :])

        gbank = bank("s2", [P, PACK, P])
        for t in range(PACK):
            turn(gbank[:, t, :], gcol[:, t : t + 1].to_broadcast([P, P]), True, True)
        grow = keep.tile([P, 2, P, 2], F32, name="grow")
        wbf.append(keep.tile([P, H * PACK], BF16, name="wbf2", align_bytes=64))
        for i, raw in ((1, raw2), (2, raw3)):
            for lo in (0, 64):
                nc.gpsimd.tensor_copy(*dealt(wbf[i], raw, 0, lo, lo + 64))

        zq = keep.tile([P, S], U32, name="zq", align_bytes=64)
        zs = keep.tile([P, S], U8, name="zs", align_bytes=64)
        units = [(c0, n, t, (0, 1, 2)) for c0, n in CHUNKS for t in range(PACK)]
        units[-1:] = [(EARLY, P, PACK - 1, (i,)) for i in range(3)]
        sums = ["s0", "s1", "y0"]
        backs = ["s2", "s3", "y1"]
        zbank = {}
        zlast = keep.tile([P, PACK, P], BF16, name="zplanes")

        def quant_z(b, zg):
            cols = slice(P * b, P * (b + 1))
            nc.vector.quantize_mx(out=zq[:, cols].bitcast(FP8X4), scales=zs[:, cols], in_=zg[:])

        def finish(b):
            zt = work.tile([P, 2, P, 2], BF16, name="zt")
            nc.vector.tensor_tensor(zt[:], zbank[b][:].rearrange("q (u e) p -> q u p e", e=2), grow[:], ALU.mult)
            words = zt[:].rearrange("q u p e -> q (u p e)").bitcast(F32)
            back = bank(backs[b], [P, 2, P])
            for u in range(2):
                turn(back[:, u, :], words[:, P * u : P * (u + 1)], True, True)
            return back

        def pack(b, back, tag):
            zg = keep.tile([P, P * PACK], BF16, name=tag, align_bytes=64)
            nc.scalar.copy(zg[:].bitcast(F32).rearrange("p (n u) -> p n u", u=2), back[:].rearrange("p u n -> p n u"))
            quant_z(b, zg)

        def gate(k):
            if k == 0:
                return "first"
            if k <= SWITCH:
                return f"ring{(k - 1) % RING}"
            if k == SWITCH + 1:
                return f"tie{SWITCH - 1}"
            return f"ring{(k - 2) % RING}"

        later = {}
        small = []
        for k, (c0, n, t, near) in enumerate(units):
            m = len(near)
            last = k == len(units) - 1
            direct = c0 == EARLY
            x = keep.tile([P, m, n], F32, name=gate(k), align_bytes=64)
            w = work.tile([P, m, n], F32, name="w", bufs=XBUFS)
            groups = [(0, 1), (2,)] if m > 1 and n == P else [(j,) for j in range(m)]
            tags = [f"ring{k % RING}", f"mid{k % 2}", f"tie{k}"] if len(groups) == 3 else [f"ring{k % RING}", f"tie{k}"][: len(groups)]
            d = [keep.tile([P, len(g), n], F32, name=tag, align_bytes=64) for g, tag in zip(groups, tags)]
            own = ybank[c0 // HALF, t // 2][:, t % 2, c0 % HALF : c0 % HALF + n]
            for g, dg in zip(groups, d):
                for e, j in enumerate(g):
                    nc.vector.tensor_copy(x[:, j, :], ywin[t][:].indirect(lists[1 + near[j]][:, c0 // 16 : (c0 + n) // 16]))
                    nc.vector.tensor_tensor(dg[:, e, :], x[:, j, :], own, ALU.subtract)
            for b, back, tag in later.get(k, []):
                pack(b, back, tag)
            parts = [slice(g[0], g[-1] + 1) for g in groups]
            for part, dg in zip(parts, d):
                nc.scalar.activation(w[:, part, :], dg[:], ACT.Square)
            if last:
                root = [keep.tile([P, P // PACK], F32, name=f"hwin{q}") for q in range(PACK)]
                for q in range(PACK):
                    nc.scalar.activation(root[q][:], w[:, 0, 32 * q : 32 * (q + 1)], ACT.Abs_reciprocal_sqrt, bias=1.0)
                for q in range(PACK):
                    nc.scalar.activation(w[:, 0, 32 * q : 32 * (q + 1)], root[q][:], ACT.Square)
            else:
                for part in parts:
                    nc.scalar.activation(w[:, part, :], w[:, part, :], ACT.Abs_reciprocal_sqrt, bias=1.0)
                for part in parts:
                    nc.scalar.activation(w[:, part, :], w[:, part, :], ACT.Square)
            r = shared.tile([P, m, n], F32, name=f"r{k}", offset=3072 * k) if k < PACK else work.tile([P, m, n], F32, name="r", bufs=XBUFS)
            gain = gcol[:, t : t + 1]
            if not direct:
                for part in parts if n > P else [slice(0, m)]:
                    nc.gpsimd.tensor_tensor(r[:, part, :], x[:, part, :], w[:, part, :], ALU.mult)
                for b in range(c0 // P, (c0 + n) // P):
                    if t == 0:
                        zbank[b] = bank(sums[b], [P, PACK, P])
                    for i in near:
                        turn(zbank[b][:, t, :], r[:, i, P * b - c0 : P * (b + 1) - c0], i == 0, i == 2)
                    if t == PACK - 1:
                        wait = WAITS[b]
                        later.setdefault(k + wait + 1, []).append((b, finish(b), f"tie{k + wait}"))
            elif m > 1:
                two = work.tile([P, n], F32, name="two")
                pair = keep.tile([P, 2, n], F32, name=f"pair{t}", align_bytes=64)
                nc.gpsimd.tensor_tensor(pair[:], x[:, 0:2, :], w[:, 0:2, :], ALU.mult)
                nc.gpsimd.tensor_tensor(two[:], pair[:, 0, :], pair[:, 1, :], ALU.add)
                nc.vector.scalar_tensor_tensor(r[:, 2, :], x[:, 2, :], gain, w[:, 2, :], ALU.mult, ALU.mult)
                nc.vector.scalar_tensor_tensor(zlast[:, t, :], two[:], gain, r[:, 2, :], ALU.mult, ALU.add)
            else:
                nc.vector.scalar_tensor_tensor(r[:, 0, :], x[:, 0, :], gain, w[:, 0, :], ALU.mult, ALU.mult)
                small.append(r)
                if near[0] == 1:
                    two = work.tile([P, n], F32, name="two")
                    nc.vector.tensor_tensor(two[:], small[0][:, 0, :], small[1][:, 0, :], ALU.add)
                if last:
                    nc.vector.tensor_tensor(zlast[:, t, :], two[:], r[:, 0, :], ALU.add)
            if k == 1:
                nc.scalar.copy(grow[:], gbank[:].rearrange("q (u e) p -> q u p e", e=2))

        wq.append(keep.tile([P, H], U32, name="ywin3", align_bytes=64))
        quant_w(1)
        zg = keep.tile([P, P * PACK], BF16, name="zlast", align_bytes=64)
        nc.vector.tensor_copy(zg[:].rearrange("p (c i t) -> p c t i", i=4, t=PACK), zlast[:].rearrange("p t (c i) -> p c t i", i=4))
        quant_z(BLOCKS - 1, zg)
        wq.append(keep.tile([P, H], U32, name="zlast", align_bytes=64))

        abank = [bank(f"s{t}", [P, EARLY]) for t in range(PACK)]
        hwin = [keep.tile([P, S], F32, name=f"hwin{t}") for t in range(PACK)]
        for t in range(PACK):
            for lo, hi in ((0, HALF), (HALF, EARLY)):
                product(abank[t][:, lo:hi], 1, t, zq[:, lo:hi], zs[:, lo:hi])
        late = bank("y0", [P, PACK, P])
        hlate = keep.tile([P, PACK, P], F32, name="g1")
        for t in range(PACK):
            product(late[:, t, :], 1, t, zq[:, EARLY:S], zs[:, EARLY:S])
        for t in range(PACK):
            nc.scalar.activation(hwin[t][:, 0:EARLY], abank[t][:], ACT.Tanh)
        for t in range(PACK):
            nc.scalar.activation(hlate[:, t, :], late[:, t, :], ACT.Tanh)
        for t in range(PACK):
            nc.vector.tensor_scalar(hwin[t][:, 0:EARLY], hwin[t][:, 0:EARLY], gcol[:, t : t + 1], None, ALU.mult)
        quant_w(2)
        for t in range(PACK):
            nc.vector.tensor_scalar(hwin[t][:, EARLY:S], hlate[:, t, :], gcol[:, t : t + 1], None, ALU.mult)

        out_v = out.rearrange("(p t) s -> p t s", t=PACK)
        obank = []
        tags = ["y1", "y2", "y3", "s0", "s1", "s2"]
        for c, (c0, n) in enumerate(TAIL):
            g = keep.tile([P, PACK, n], GT, name=f"g{c % 2}")
            for t in range(PACK):
                nc.vector.tensor_copy(g[:, t, :], hwin[t][:].indirect(l_mv[:, c0 // 16 : (c0 + n) // 16]))
            for b in range(c0 // P, (c0 + n) // P):
                final = b == BLOCKS - 1
                z2 = work.tile([P, P * PACK], BF16, name="z2", align_bytes=64)
                weave = nc.vector.tensor_copy if final else nc.scalar.copy
                weave(z2[:].rearrange("p (c i t) -> p c t i", i=4, t=PACK),
                      g[:, :, P * b - c0 : P * (b + 1) - c0].rearrange("p t (c i) -> p c t i", i=4))
                q2 = work.tile([P, P], U32, name="q2", align_bytes=64)
                s2 = work.tile([P, P], U8, name="s2", align_bytes=64)
                nc.vector.quantize_mx(out=q2[:].bitcast(FP8X4), scales=s2[:], in_=z2[:])
                rows = 2 if final else PACK
                for t0 in range(0, PACK, rows):
                    ob = bank(tags[len(obank)], [P, rows, P])
                    obank.append((ob, slice(t0, t0 + rows), slice(P * b, P * (b + 1))))
                    for t in range(rows):
                        product(ob[:, t, :], 2, t0 + t, q2[:], s2[:])
        for ob, planes, cols in obank:
            o = work.tile([P, planes.stop - planes.start, cols.stop - cols.start], F32, name="o", bufs=6)
            nc.vector.tensor_tensor(o[:], ob[:], res_sb[:, planes, cols], ALU.add)
            nc.sync.dma_start(out_v[:, planes, cols], o[:])
